import numpy as np
import ml_dtypes


def mxq(x, axis, fmt="e4m3"):
    dtype, down = {"e4m3": (ml_dtypes.float8_e4m3fn, 7), "e5m2": (ml_dtypes.float8_e5m2, 14)}[fmt]
    v = np.moveaxis(np.asarray(x, np.float32).astype(ml_dtypes.bfloat16).astype(np.float64), axis, -1)
    blocks = v.reshape(v.shape[:-1] + (-1, 32))
    amax = np.abs(blocks).max(-1, keepdims=True)
    byte = np.maximum(np.where(amax > 0, np.frexp(amax)[1] - 1 + 127, 0) - down, 1)
    scale = np.exp2(byte - 127.0)
    codes = (blocks / scale).astype(np.float32).astype(dtype).astype(np.float64)
    return np.moveaxis((codes * scale).reshape(v.shape), -1, axis)


WIDE = False


def mx_kscale(k):
    if not WIDE:
        return np.ones(k)
    levels = np.array([30, -30])
    if k % 512:
        return np.exp2(np.random.permutation(np.resize(levels, k // 32))).repeat(32)
    a = np.empty((k // 512, 16))
    for p in range(k // 512):
        a[p, :8] = np.random.permutation(np.resize(levels, 8))
        for g in range(8):
            far = levels[np.abs(levels - a[p, g]) >= 10]
            a[p, g + 8] = far[np.random.randint(len(far))]
    return np.exp2(a.ravel()).repeat(32)


BF16 = ml_dtypes.bfloat16


def bf(x):
    return np.asarray(x, np.float32).astype(BF16)


def f64(x):
    return np.asarray(x).astype(np.float64)


E2M1 = np.array([0.0, 0.5, 1.0, 1.5, 2.0, 3.0, 4.0, 6.0, -0.0, -0.5, -1.0, -1.5, -2.0, -3.0, -4.0, -6.0])


def pack_weight(w, fmt):
    k, n = w.shape
    w = f64(bf(w)).reshape(k // 32, 32, n)
    amax = np.abs(w).max(1)
    if fmt in ("e4m3", "e5m2"):
        byte = np.frexp(amax)[1] - 1 + 127 - (7 if fmt == "e4m3" else 14)
    else:
        mant, ex = np.frexp(amax / 6.0)
        byte = np.where(mant > 0.5, ex, ex - 1) + 127
    byte = np.clip(np.where(amax > 0, byte, 1), 1, 254)
    scaled = (w * np.exp2(127.0 - byte)[:, None, :]).reshape(k, n).astype(np.float32)
    by_word = np.ascontiguousarray(scaled.reshape(k // 512, 128, 4, n).transpose(0, 1, 3, 2))
    if fmt in ("e4m3", "e5m2"):
        words = by_word.astype(ml_dtypes.float8_e4m3fn if fmt == "e4m3" else ml_dtypes.float8_e5m2).view(np.uint8)
    else:
        c = by_word.astype(ml_dtypes.float4_e2m1fn).view(np.uint8) & 0xF
        words = c[..., 0::2] | (c[..., 1::2] << 4)
    return np.ascontiguousarray(words), np.ascontiguousarray(byte.astype(np.uint8).reshape(k // 512, 16, n))


def unpack_weight(words, scales, fmt):
    g, p, n, _ = words.shape
    if fmt in ("e4m3", "e5m2"):
        vals = np.ascontiguousarray(words).view(ml_dtypes.float8_e4m3fn if fmt == "e4m3" else ml_dtypes.float8_e5m2).astype(np.float64)
    else:
        nib = np.empty((g, p, n, 4), np.uint8)
        nib[..., 0::2] = words & 0xF
        nib[..., 1::2] = words >> 4
        vals = E2M1[nib]
    vals = vals * np.repeat(np.exp2(scales.astype(np.float64) - 127.0), 8, axis=1)[..., None]
    return vals.transpose(0, 1, 3, 2).reshape(g * 512, n)

def planes(Y):
    n, m = Y.shape
    b = f64(bf(Y)).reshape(n // 32, 32, m)
    amax = np.abs(b).max(1)
    byte = np.clip(np.where(amax > 0, np.frexp(amax)[1] - 1 + 127 - 7, 1), 1, 254)
    codes = (b * np.exp2(127.0 - byte)[:, None, :]).reshape(n, m).astype(np.float32).astype(ml_dtypes.float8_e4m3fn).view(np.uint8)
    words = codes.reshape(n // 512, 128, 4, m).transpose(0, 1, 3, 2)
    return np.ascontiguousarray(words), np.ascontiguousarray(byte.astype(np.uint8).reshape(n // 512, 16, m))


A, K, U, R, S = 2048, 4096, 512, 1024, 8

def cnoise(rows, cols):
    return np.random.randn(rows, cols) + 1j * np.random.randn(rows, cols)

def setup_inputs():
    phase = 2 * np.pi * np.random.rand(A, S)
    steer = np.cos(phase) + 1j * np.sin(phase)
    gain = cnoise(S, U)
    paths = sum(steer[:, j, None] * gain[None, j] for j in range(S)) / np.sqrt(S)
    shadow = np.exp(0.9 * np.random.randn(A, U) - 0.81)
    H = np.sqrt(0.75 / A) * (paths + shadow * cnoise(A, U))
    Hr = np.concatenate([np.concatenate([H.real, -H.imag], axis=1),
                         np.concatenate([H.imag, H.real], axis=1)], axis=0)
    s = mx_kscale(K)
    h_words, h_scales = pack_weight(Hr * s[:, None], "e5m2")
    return {"h_words": h_words, "h_scales": h_scales,
            "h_stack": bf(Hr[:, :U] / s[:, None]),
            "load": bf(2.0 * np.exp(0.3 * np.random.randn(U))),
            "col_scale": bf(np.exp(0.8 * np.random.randn(U)))}

def reference(h_words, h_scales, h_stack, load, col_scale):
    Hr = unpack_weight(h_words, h_scales, "e5m2")
    Hs = mxq(f64(h_stack), 0, "e4m3")
    gram = Hr.T @ Hs
    y = (gram + np.eye(R, U) * f64(load)) * f64(col_scale)
    Y = y.T
    words, scales = planes(Y)
    return y, words, scales

@@ -1,0 +1,266 @@
+from contextlib import ExitStack
+
+import concourse.mybir as mybir
+from concourse.masks import make_identity
+
+K, U, R = 4096, 512, 1024
+FLOPS = 2 * K * U * R
+
+F32 = mybir.dt.float32
+BF16 = mybir.dt.bfloat16
+I32 = mybir.dt.int32
+U32 = mybir.dt.uint32
+U8 = mybir.dt.uint8
+E4M3X4 = mybir.dt.float8_e4m3fn_x4
+E5M2X4 = mybir.dt.float8_e5m2_x4
+MULT = mybir.AluOpType.mult
+ADD = mybir.AluOpType.add
+
+P = 128
+PACK = 4
+PASSES = K // (P * PACK)
+TILES = R // P
+WIDE = 6
+EARLY = 2
+VECTOR_COLS = 336
+ORDER = (0, 1, 2, 3, 4, 5, 6, 7)
+
+
+def tile_mimo_loaded_gram_k2_kernel(tc, h_words, h_scales, h_stack, load, col_scale, out_0, out_1, out_2):
+    nc = tc.nc
+    with ExitStack() as ctx:
+        keep = ctx.enter_context(tc.tile_pool(name="keep", bufs=1))
+        stage = ctx.enter_context(tc.tile_pool(name="stage", bufs=3))
+        psum = ctx.enter_context(tc.psum_pool(name="psum", bufs=1))
+        ctx.enter_context(tc.manual_schedule())
+
+        cs_in = keep.tile([P, PACK], BF16, name="cs_in")
+        load_in = keep.tile([P, PACK], BF16, name="load_in")
+        nc.scalar.dma_start(out=cs_in[:], in_=col_scale.rearrange("(p c) -> p c", c=PACK))
+        nc.scalar.dma_start(out=load_in[:], in_=load.rearrange("(p c) -> p c", c=PACK))
+
+        ident_bf = keep.tile([P, P], BF16, name="ident_bf")
+        ident = keep.tile([P, P], F32, name="ident")
+        make_identity(nc, ident_bf[:])
+        nc.scalar.copy(out=ident[:], in_=ident_bf[:])
+
+        sc_early = keep.tile([P, EARLY, R], U8, name="sc_early", align_bytes=64)
+        sc_late = keep.tile([P, PASSES - EARLY, R], U8, name="sc_late", align_bytes=64)
+        nc.vector.memset(sc_early[:].bitcast(I32), 0)
+        nc.vector.memset(sc_late[:].bitcast(I32), 0)
+
+        raw = {}
+        hw = {}
+        hw_tail = {}
+
+        def load_stack(g):
+            raw[g] = keep.tile([P, PACK, U], BF16, name="raw%d" % g)
+            nc.sync.dma_start(out=raw[g][:], in_=h_stack[512 * g : 512 * (g + 1), :].rearrange("(p t) u -> p t u", t=PACK))
+
+        def load_words(g):
+            hw[g] = keep.tile([P, R], U32, name="hw%d" % g, align_bytes=64)
+            nc.sync.dma_start(out=hw[g][:].bitcast(I32), in_=h_words[g].rearrange("p n t -> p (n t)").bitcast(I32))
+
+        def load_tail(m):
+            j = ORDER[2 * m]
+            hw_tail[m] = keep.tile([P, PASSES - WIDE, 2 * P], U32, name="hwt%d" % m, align_bytes=64)
+            src = h_words[WIDE:PASSES, :, P * j : P * (j + 2), :].rearrange("g p n t -> p g (n t)").bitcast(I32)
+            nc.sync.dma_start(out=hw_tail[m][:].bitcast(I32), in_=src)
+
+        def load_scales(plane, g0, g1):
+            rows = h_scales[g0:g1].rearrange("g (q r) n -> r q g n", r=4)
+            for r in range(4):
+                nc.sync.dma_start(out=plane[r:P:32, :, :].bitcast(I32), in_=rows[r].bitcast(I32))
+
+        load_stack(0)
+        load_words(0)
+        load_scales(sc_early, 0, EARLY)
+        load_stack(1)
+        load_words(1)
+        load_scales(sc_late, EARLY, PASSES)
+        for g in range(2, WIDE - 1):
+            load_stack(g)
+            load_words(g)
+        load_stack(WIDE - 1)
+        load_stack(WIDE)
+        load_words(WIDE - 1)
+        load_stack(WIDE + 1)
+        for m in range(TILES // 2):
+            load_tail(m)
+
+        cs32 = keep.tile([P, PACK], F32, name="cs32")
+        lc32 = keep.tile([P, PACK], F32, name="lc32")
+        nc.gpsimd.tensor_copy(out=cs32[:], in_=cs_in[:])
+        nc.gpsimd.tensor_tensor(out=lc32[:], in0=cs_in[:], in1=load_in[:], op=MULT)
+        cs_ps = psum.tile([P, PACK, P], F32, name="cs_ps", tag="bank6")
+        lc_ps = psum.tile([P, PACK, P], F32, name="lc_ps", tag="bank7")
+        for c in range(PACK):
+            nc.tensor.transpose(cs_ps[:, c, :], cs32[:, c : c + 1].to_broadcast([P, P]), ident[:])
+        for c in range(PACK):
+            nc.tensor.transpose(lc_ps[:, c, :], lc32[:, c : c + 1].to_broadcast([P, P]), ident[:])
+        cs_all = keep.tile([P, U], F32, name="cs_all")
+        diag = keep.tile([P, PACK, P], F32, name="diag")
+
+        codes = {}
+        scales = {}
+
+        def quantise_stack(g):
+            grouped = stage.tile([P, U, PACK], BF16, name="grouped", align_bytes=64)
+            for eng_copy, lo, hi in ((nc.vector.tensor_copy, 0, VECTOR_COLS), (nc.scalar.copy, VECTOR_COLS, U)):
+                eng_copy(
+                    out=grouped[:, lo:hi, :].rearrange("p (c i) t -> p c t i", i=4),
+                    in_=raw[g][:, :, lo:hi].rearrange("p t (c i) -> p c t i", i=4),
+                )
+            codes[g] = keep.tile([P, U], U32, name="codes%d" % g, align_bytes=64)
+            scales[g] = keep.tile([P, U], U8, name="scales%d" % g, align_bytes=64)
+            nc.vector.quantize_mx(out=codes[g][:].bitcast(E4M3X4), scales=scales[g][:], in_=grouped[:].rearrange("p u t -> p (u t)"))
+
+        acc = {}
+
+        def multiply(s, g):
+            j = ORDER[s]
+            if g == 0:
+                acc[s] = psum.tile([P, U], F32, name="acc%d" % s, tag="bank%d" % s)
+            if g < WIDE:
+                words = hw[g][:, P * j : P * (j + 1)]
+            else:
+                words = hw_tail[s // 2][:, g - WIDE, P * (s % 2) : P * (s % 2 + 1)]
+            plane = sc_early[:, g, :] if g < EARLY else sc_late[:, g - EARLY, :]
+            nc.tensor.matmul_mx(
+                out=acc[s][:],
+                lhsT=words.bitcast(E5M2X4),
+                lhsT_scale=plane[:, P * j : P * (j + 1)],
+                rhs=codes[g][:].bitcast(E4M3X4),
+                rhs_scale=scales[g][:],
+                start=(g == 0),
+                stop=(g == PASSES - 1),
+            )
+
+        quantise_stack(0)
+        nc.scalar.copy(out=cs_all[:].rearrange("p (q c) -> p q c", c=PACK), in_=cs_ps[:].rearrange("p c q -> p q c"))
+        nc.vector.tensor_tensor(
+            out=diag[:].rearrange("p j (q c) -> p j q c", c=PACK),
+            in0=lc_ps[:].rearrange("p c (j q) -> p j q c", j=PACK),
+            in1=ident[:].rearrange("p (q c) -> p q c", c=PACK).unsqueeze(1).to_broadcast([P, PACK, P // PACK, PACK]),
+            op=MULT,
+        )
+        for g in range(WIDE):
+            if g > 0:
+                quantise_stack(g)
+            for s in range(TILES):
+                multiply(s, g)
+        for g in range(WIDE, PASSES):
+            quantise_stack(g)
+
+        y = {}
+        y_bf = {}
+        out_codes = keep.tile([P, R], U32, name="out_codes", align_bytes=64)
+        out_scales = keep.tile([P, R], U8, name="out_scales", align_bytes=64)
+        turned = {}
+        packed = {}
+
+        def finish(s):
+            for g in range(WIDE, PASSES):
+                multiply(s, g)
+
+        def scale(s):
+            j = ORDER[s]
+            y[s] = keep.tile([P, U], F32, name="y%d" % s)
+            nc.vector.tensor_tensor(out=y[s][:], in0=acc[s][:], in1=cs_all[:], op=MULT)
+            if j < PACK:
+                block = y[s][:, P * j : P * (j + 1)]
+                nc.gpsimd.tensor_tensor(out=block, in0=block, in1=diag[:, j, :], op=ADD)
+
+        def store_y(s):
+            j = ORDER[s]
+            nc.sync.dma_start(out=out_0[P * j : P * (j + 1), :], in_=y[s][:])
+
+        def by_pairs(ap):
+            return ap.rearrange("p (q e b) -> p e q b", e=2, b=2)
+
+        def round_y(s, eng_copy):
+            y_bf[s] = keep.tile([P, U], BF16, name="ybf%d" % s)
+            eng_copy(out=y_bf[s][:].rearrange("p (e q b) -> p e q b", e=2, b=2), in_=by_pairs(y[s][:]))
+
+        def round_from_psum(s):
+            y_bf[s] = keep.tile([P, U], BF16, name="ybf%d" % s)
+            nc.vector.tensor_tensor(
+                out=y_bf[s][:].rearrange("p (e q b) -> p e q b", e=2, b=2), in0=by_pairs(acc[s][:]), in1=by_pairs(cs_all[:]), op=MULT
+            )
+
+        def turn(m):
+            turned[m] = psum.tile([P, 2, 2, P], F32, name="turned%d" % m, tag="bank%d" % (2 * m))
+            for h in range(2):
+                words = y_bf[2 * m + h][:].bitcast(F32)
+                for e in range(2):
+                    nc.tensor.transpose(turned[m][:, h, e, :], words[:, P * e : P * (e + 1)], ident[:])
+
+        def pack(m, eng_copy):
+            packed[m] = keep.tile([P, 2, P, 2], F32, name="packed%d" % m, align_bytes=64)
+            eng_copy(out=packed[m][:], in_=turned[m][:].rearrange("p h e i -> p h i e"))
+
+        def quantise_y(m):
+            cols = slice(P * ORDER[2 * m], P * (ORDER[2 * m] + 2))
+            nc.vector.quantize_mx(
+                out=out_codes[:, cols].bitcast(E4M3X4),
+                scales=out_scales[:, cols],
+                in_=packed[m][:].rearrange("p h i e -> p (h i e)").bitcast(BF16),
+            )
+
+        def store_codes(m):
+            cols = slice(P * ORDER[2 * m], P * (ORDER[2 * m] + 2))
+            dst = out_1[0].rearrange("p n t -> p (n t)").bitcast(I32)
+            nc.sync.dma_start(out=dst[:, cols], in_=out_codes[:, cols].bitcast(I32))
+
+        finish(0)
+        finish(1)
+        scale(0)
+        finish(2)
+        scale(1)
+        round_y(0, nc.scalar.copy)
+        store_y(0)
+        finish(3)
+        scale(2)
+        round_y(1, nc.scalar.copy)
+        store_y(1)
+        finish(4)
+        scale(3)
+        round_y(2, nc.scalar.copy)
+        store_y(2)
+        finish(5)
+        scale(4)
+        round_y(3, nc.scalar.copy)
+        store_y(3)
+        store_y(4)
+        finish(6)
+        scale(5)
+        round_y(4, nc.scalar.copy)
+        store_y(5)
+        finish(7)
+        scale(6)
+        round_y(5, nc.scalar.copy)
+        store_y(6)
+        scale(7)
+        store_y(7)
+        round_y(6, nc.scalar.copy)
+        round_y(7, nc.vector.tensor_copy)
+        turn(0)
+        turn(1)
+        turn(2)
+        turn(3)
+        pack(0, nc.vector.tensor_copy)
+        pack(1, nc.scalar.copy)
+        pack(2, nc.scalar.copy)
+        pack(3, nc.scalar.copy)
+        quantise_y(1)
+        store_codes(1)
+        quantise_y(0)
+        store_codes(0)
+        quantise_y(2)
+        store_codes(2)
+        quantise_y(3)
+        store_codes(3)
+        rows = out_2[0].rearrange("(q r) n -> r q n", r=4)
+        for r in range(4):
+            queue = nc.sync if r < 2 else nc.scalar
+            queue.dma_start(out=rows[r].bitcast(I32), in_=out_scales[r:P:32, :].bitcast(I32))

@@ -62,9 +62,9 @@ def tile_mimo_loaded_gram_k2_kernel(tc, h_words, h_scales, h_stack, load, col_sc
             nc.sync.dma_start(out=hw[g][:].bitcast(I32), in_=h_words[g].rearrange("p n t -> p (n t)").bitcast(I32))
 
         def load_tail(m):
-            j = ORDER[2 * m]
-            hw_tail[m] = keep.tile([P, PASSES - WIDE, 2 * P], U32, name="hwt%d" % m, align_bytes=64)
-            src = h_words[WIDE:PASSES, :, P * j : P * (j + 2), :].rearrange("g p n t -> p g (n t)").bitcast(I32)
+            j = 4 * m
+            hw_tail[m] = keep.tile([P, PASSES - WIDE, 4 * P], U32, name="hwt%d" % m, align_bytes=64)
+            src = h_words[WIDE:PASSES, :, P * j : P * (j + 4), :].rearrange("g p n t -> p g (n t)").bitcast(I32)
             nc.sync.dma_start(out=hw_tail[m][:].bitcast(I32), in_=src)
 
         def load_scales(plane, g0, g1):
@@ -85,7 +85,7 @@ def tile_mimo_loaded_gram_k2_kernel(tc, h_words, h_scales, h_stack, load, col_sc
         load_stack(WIDE)
         load_words(WIDE - 1)
         load_stack(WIDE + 1)
-        for m in range(TILES // 2):
+        for m in range(2):
             load_tail(m)
 
         cs32 = keep.tile([P, PACK], F32, name="cs32")
@@ -108,8 +108,8 @@ def tile_mimo_loaded_gram_k2_kernel(tc, h_words, h_scales, h_stack, load, col_sc
             grouped = stage.tile([P, U, PACK], BF16, name="grouped", align_bytes=64)
             for eng_copy, lo, hi in ((nc.vector.tensor_copy, 0, VECTOR_COLS), (nc.scalar.copy, VECTOR_COLS, U)):
                 eng_copy(
-                    out=grouped[:, lo:hi, :].rearrange("p (c i) t -> p c t i", i=4),
-                    in_=raw[g][:, :, lo:hi].rearrange("p t (c i) -> p c t i", i=4),
+                    out=grouped[:, lo:hi, :],
+                    in_=raw[g][:, :, lo:hi].rearrange("p t u -> p u t"),
                 )
             codes[g] = keep.tile([P, U], U32, name="codes%d" % g, align_bytes=64)
             scales[g] = keep.tile([P, U], U8, name="scales%d" % g, align_bytes=64)
@@ -124,7 +124,7 @@ def tile_mimo_loaded_gram_k2_kernel(tc, h_words, h_scales, h_stack, load, col_sc
             if g < WIDE:
                 words = hw[g][:, P * j : P * (j + 1)]
             else:
-                words = hw_tail[s // 2][:, g - WIDE, P * (s % 2) : P * (s % 2 + 1)]
+                words = hw_tail[s // 4][:, g - WIDE, P * (s % 4) : P * (s % 4 + 1)]
             plane = sc_early[:, g, :] if g < EARLY else sc_late[:, g - EARLY, :]
             nc.tensor.matmul_mx(
                 out=acc[s][:],
@@ -157,7 +157,7 @@ def tile_mimo_loaded_gram_k2_kernel(tc, h_words, h_scales, h_stack, load, col_sc
         out_codes = keep.tile([P, R], U32, name="out_codes", align_bytes=64)
         out_scales = keep.tile([P, R], U8, name="out_scales", align_bytes=64)
         turned = {}
-        packed = {}
+        packed = keep.tile([P, 2 * R], F32, name="packed", align_bytes=64)
 
         def finish(s):
             for g in range(WIDE, PASSES):
@@ -196,19 +196,16 @@ def tile_mimo_loaded_gram_k2_kernel(tc, h_words, h_scales, h_stack, load, col_sc
                     nc.tensor.transpose(turned[m][:, h, e, :], words[:, P * e : P * (e + 1)], ident[:])
 
         def pack(m, eng_copy):
-            packed[m] = keep.tile([P, 2, P, 2], F32, name="packed%d" % m, align_bytes=64)
-            eng_copy(out=packed[m][:], in_=turned[m][:].rearrange("p h e i -> p h i e"))
+            dst = packed[:, 4 * P * m : 4 * P * (m + 1)].rearrange("p (h i e) -> p h i e", h=2, e=2)
+            eng_copy(out=dst, in_=turned[m][:].rearrange("p h e i -> p h i e"))
 
-        def quantise_y(m):
-            cols = slice(P * ORDER[2 * m], P * (ORDER[2 * m] + 2))
+        def quantise_y(j0, j1):
+            cols = slice(P * j0, P * j1)
             nc.vector.quantize_mx(
                 out=out_codes[:, cols].bitcast(E4M3X4),
                 scales=out_scales[:, cols],
-                in_=packed[m][:].rearrange("p h i e -> p (h i e)").bitcast(BF16),
+                in_=packed[:, 2 * P * j0 : 2 * P * j1].bitcast(BF16),
             )
-
-        def store_codes(m):
-            cols = slice(P * ORDER[2 * m], P * (ORDER[2 * m] + 2))
             dst = out_1[0].rearrange("p n t -> p (n t)").bitcast(I32)
             nc.sync.dma_start(out=dst[:, cols], in_=out_codes[:, cols].bitcast(I32))
 
@@ -242,24 +239,19 @@ def tile_mimo_loaded_gram_k2_kernel(tc, h_words, h_scales, h_stack, load, col_sc
         store_y(6)
         scale(7)
         store_y(7)
-        round_y(6, nc.scalar.copy)
+        round_y(6, nc.vector.tensor_copy)
         round_y(7, nc.vector.tensor_copy)
         turn(0)
         turn(1)
         turn(2)
         turn(3)
-        pack(0, nc.vector.tensor_copy)
+        pack(0, nc.scalar.copy)
         pack(1, nc.scalar.copy)
-        pack(2, nc.scalar.copy)
+        pack(2, nc.vector.tensor_copy)
         pack(3, nc.scalar.copy)
-        quantise_y(1)
-        store_codes(1)
-        quantise_y(0)
-        store_codes(0)
-        quantise_y(2)
-        store_codes(2)
-        quantise_y(3)
-        store_codes(3)
+        quantise_y(0, 4)
+        quantise_y(4, 6)
+        quantise_y(6, 8)
         rows = out_2[0].rearrange("(q r) n -> r q n", r=4)
         for r in range(4):
             queue = nc.sync if r < 2 else nc.scalar

@@ -21,7 +21,7 @@ PACK = 4
 PASSES = K // (P * PACK)
 TILES = R // P
 WIDE = 6
-EARLY = 2
+SCALE_RUNS = ((0, 2), (2, 5), (5, 8))
 VECTOR_COLS = 336
 ORDER = (0, 1, 2, 3, 4, 5, 6, 7)
 
@@ -44,10 +44,10 @@ def tile_mimo_loaded_gram_k2_kernel(tc, h_words, h_scales, h_stack, load, col_sc
         make_identity(nc, ident_bf[:])
         nc.scalar.copy(out=ident[:], in_=ident_bf[:])
 
-        sc_early = keep.tile([P, EARLY, R], U8, name="sc_early", align_bytes=64)
-        sc_late = keep.tile([P, PASSES - EARLY, R], U8, name="sc_late", align_bytes=64)
-        nc.vector.memset(sc_early[:].bitcast(I32), 0)
-        nc.vector.memset(sc_late[:].bitcast(I32), 0)
+        planes = {}
+        for g0, g1 in SCALE_RUNS:
+            planes[g0] = keep.tile([P, g1 - g0, R], U8, name="plane%d" % g0, align_bytes=64)
+            nc.vector.memset(planes[g0][:].bitcast(I32), 0)
 
         raw = {}
         hw = {}
@@ -57,9 +57,11 @@ def tile_mimo_loaded_gram_k2_kernel(tc, h_words, h_scales, h_stack, load, col_sc
             raw[g] = keep.tile([P, PACK, U], BF16, name="raw%d" % g)
             nc.sync.dma_start(out=raw[g][:], in_=h_stack[512 * g : 512 * (g + 1), :].rearrange("(p t) u -> p t u", t=PACK))
 
-        def load_words(g):
-            hw[g] = keep.tile([P, R], U32, name="hw%d" % g, align_bytes=64)
-            nc.sync.dma_start(out=hw[g][:].bitcast(I32), in_=h_words[g].rearrange("p n t -> p (n t)").bitcast(I32))
+        def load_words(g, lo=0, hi=R):
+            if lo == 0:
+                hw[g] = keep.tile([P, R], U32, name="hw%d" % g, align_bytes=64)
+            src = h_words[g].rearrange("p n t -> p (n t)").bitcast(I32)
+            nc.sync.dma_start(out=hw[g][:, lo:hi].bitcast(I32), in_=src[:, lo:hi])
 
         def load_tail(m):
             j = 4 * m
@@ -74,17 +76,18 @@ def tile_mimo_loaded_gram_k2_kernel(tc, h_words, h_scales, h_stack, load, col_sc
 
         load_stack(0)
         load_words(0)
-        load_scales(sc_early, 0, EARLY)
         load_stack(1)
+        for g0, g1 in SCALE_RUNS:
+            load_scales(planes[g0], g0, g1)
         load_words(1)
-        load_scales(sc_late, EARLY, PASSES)
         for g in range(2, WIDE - 1):
             load_stack(g)
             load_words(g)
         load_stack(WIDE - 1)
         load_stack(WIDE)
-        load_words(WIDE - 1)
+        load_words(WIDE - 1, 0, R // 2)
         load_stack(WIDE + 1)
+        load_words(WIDE - 1, R // 2, R)
         for m in range(2):
             load_tail(m)
 
@@ -125,7 +128,8 @@ def tile_mimo_loaded_gram_k2_kernel(tc, h_words, h_scales, h_stack, load, col_sc
                 words = hw[g][:, P * j : P * (j + 1)]
             else:
                 words = hw_tail[s // 4][:, g - WIDE, P * (s % 4) : P * (s % 4 + 1)]
-            plane = sc_early[:, g, :] if g < EARLY else sc_late[:, g - EARLY, :]
+            first = max(g0 for g0, g1 in SCALE_RUNS if g0 <= g)
+            plane = planes[first][:, g - first, :]
             nc.tensor.matmul_mx(
                 out=acc[s][:],
                 lhsT=words.bitcast(E5M2X4),

@@ -21,9 +21,9 @@ PACK = 4
 PASSES = K // (P * PACK)
 TILES = R // P
 WIDE = 6
-SCALE_RUNS = ((0, 2), (2, 5), (5, 8))
+SCALE_RUNS = ((0, 2), (2, 4), (4, 6), (6, 8))
 VECTOR_COLS = 336
-ORDER = (0, 1, 2, 3, 4, 5, 6, 7)
+ORDER = (4, 5, 2, 3, 0, 1, 6, 7)
 
 
 def tile_mimo_loaded_gram_k2_kernel(tc, h_words, h_scales, h_stack, load, col_scale, out_0, out_1, out_2):
@@ -63,11 +63,12 @@ def tile_mimo_loaded_gram_k2_kernel(tc, h_words, h_scales, h_stack, load, col_sc
             src = h_words[g].rearrange("p n t -> p (n t)").bitcast(I32)
             nc.sync.dma_start(out=hw[g][:, lo:hi].bitcast(I32), in_=src[:, lo:hi])
 
-        def load_tail(m):
-            j = 4 * m
-            hw_tail[m] = keep.tile([P, PASSES - WIDE, 4 * P], U32, name="hwt%d" % m, align_bytes=64)
-            src = h_words[WIDE:PASSES, :, P * j : P * (j + 4), :].rearrange("g p n t -> p g (n t)").bitcast(I32)
-            nc.sync.dma_start(out=hw_tail[m][:].bitcast(I32), in_=src)
+        def load_tail(j0, j1):
+            words = keep.tile([P, PASSES - WIDE, P * (j1 - j0)], U32, name="hwt%d" % j0, align_bytes=64)
+            src = h_words[WIDE:PASSES, :, P * j0 : P * j1, :].rearrange("g p n t -> p g (n t)").bitcast(I32)
+            nc.sync.dma_start(out=words[:].bitcast(I32), in_=src)
+            for j in range(j0, j1):
+                hw_tail[j] = words[:, :, P * (j - j0) : P * (j - j0 + 1)]
 
         def load_scales(plane, g0, g1):
             rows = h_scales[g0:g1].rearrange("g (q r) n -> r q g n", r=4)
@@ -77,7 +78,7 @@ def tile_mimo_loaded_gram_k2_kernel(tc, h_words, h_scales, h_stack, load, col_sc
         load_stack(0)
         load_words(0)
         load_stack(1)
-        for g0, g1 in SCALE_RUNS:
+        for g0, g1 in SCALE_RUNS[:-1]:
             load_scales(planes[g0], g0, g1)
         load_words(1)
         for g in range(2, WIDE - 1):
@@ -85,16 +86,16 @@ def tile_mimo_loaded_gram_k2_kernel(tc, h_words, h_scales, h_stack, load, col_sc
             load_words(g)
         load_stack(WIDE - 1)
         load_stack(WIDE)
-        load_words(WIDE - 1, 0, R // 2)
+        load_words(WIDE - 1)
         load_stack(WIDE + 1)
-        load_words(WIDE - 1, R // 2, R)
-        for m in range(2):
-            load_tail(m)
+        load_scales(planes[WIDE], WIDE, PASSES)
+        for s in range(0, TILES, 2):
+            load_tail(ORDER[s], ORDER[s] + 2)
 
         cs32 = keep.tile([P, PACK], F32, name="cs32")
         lc32 = keep.tile([P, PACK], F32, name="lc32")
-        nc.gpsimd.tensor_copy(out=cs32[:], in_=cs_in[:])
-        nc.gpsimd.tensor_tensor(out=lc32[:], in0=cs_in[:], in1=load_in[:], op=MULT)
+        nc.vector.tensor_copy(out=cs32[:], in_=cs_in[:])
+        nc.vector.tensor_tensor(out=lc32[:], in0=cs_in[:], in1=load_in[:], op=MULT)
         cs_ps = psum.tile([P, PACK, P], F32, name="cs_ps", tag="bank6")
         lc_ps = psum.tile([P, PACK, P], F32, name="lc_ps", tag="bank7")
         for c in range(PACK):
@@ -109,14 +110,24 @@ def tile_mimo_loaded_gram_k2_kernel(tc, h_words, h_scales, h_stack, load, col_sc
 
         def quantise_stack(g):
             grouped = stage.tile([P, U, PACK], BF16, name="grouped", align_bytes=64)
-            for eng_copy, lo, hi in ((nc.vector.tensor_copy, 0, VECTOR_COLS), (nc.scalar.copy, VECTOR_COLS, U)):
+            shares = (
+                (nc.vector.tensor_copy, 0, U // 2),
+                (nc.vector.tensor_copy, U // 2, VECTOR_COLS),
+                (nc.scalar.copy, VECTOR_COLS, U),
+            )
+            for eng_copy, lo, hi in shares:
                 eng_copy(
-                    out=grouped[:, lo:hi, :],
-                    in_=raw[g][:, :, lo:hi].rearrange("p t u -> p u t"),
+                    out=grouped[:, lo:hi, :].rearrange("p (c i) t -> p c t i", i=4),
+                    in_=raw[g][:, :, lo:hi].rearrange("p t (c i) -> p c t i", i=4),
                 )
             codes[g] = keep.tile([P, U], U32, name="codes%d" % g, align_bytes=64)
             scales[g] = keep.tile([P, U], U8, name="scales%d" % g, align_bytes=64)
-            nc.vector.quantize_mx(out=codes[g][:].bitcast(E4M3X4), scales=scales[g][:], in_=grouped[:].rearrange("p u t -> p (u t)"))
+            for lo, hi in ((0, U // 2), (U // 2, U)):
+                nc.vector.quantize_mx(
+                    out=codes[g][:, lo:hi].bitcast(E4M3X4),
+                    scales=scales[g][:, lo:hi],
+                    in_=grouped[:, lo:hi, :].rearrange("p u t -> p (u t)"),
+                )
 
         acc = {}
 
@@ -127,7 +138,7 @@ def tile_mimo_loaded_gram_k2_kernel(tc, h_words, h_scales, h_stack, load, col_sc
             if g < WIDE:
                 words = hw[g][:, P * j : P * (j + 1)]
             else:
-                words = hw_tail[s // 4][:, g - WIDE, P * (s % 4) : P * (s % 4 + 1)]
+                words = hw_tail[j][:, g - WIDE, :]
             first = max(g0 for g0, g1 in SCALE_RUNS if g0 <= g)
             plane = planes[first][:, g - first, :]
             nc.tensor.matmul_mx(
@@ -151,12 +162,13 @@ def tile_mimo_loaded_gram_k2_kernel(tc, h_words, h_scales, h_stack, load, col_sc
         for g in range(WIDE):
             if g > 0:
                 quantise_stack(g)
-            for s in range(TILES):
-                multiply(s, g)
+            for j in range(TILES):
+                multiply(ORDER.index(j), g)
         for g in range(WIDE, PASSES):
             quantise_stack(g)
 
-        y = {}
+        y_all = keep.tile([P, R // P * U], F32, name="y_all")
+        y = {s: y_all[:, U * ORDER[s] : U * (ORDER[s] + 1)] for s in range(TILES)}
         y_bf = {}
         out_codes = keep.tile([P, R], U32, name="out_codes", align_bytes=64)
         out_scales = keep.tile([P, R], U8, name="out_scales", align_bytes=64)
@@ -169,22 +181,24 @@ def tile_mimo_loaded_gram_k2_kernel(tc, h_words, h_scales, h_stack, load, col_sc
 
         def scale(s):
             j = ORDER[s]
-            y[s] = keep.tile([P, U], F32, name="y%d" % s)
-            nc.vector.tensor_tensor(out=y[s][:], in0=acc[s][:], in1=cs_all[:], op=MULT)
+            nc.vector.tensor_tensor(out=y[s], in0=acc[s][:], in1=cs_all[:], op=MULT)
             if j < PACK:
                 block = y[s][:, P * j : P * (j + 1)]
                 nc.gpsimd.tensor_tensor(out=block, in0=block, in1=diag[:, j, :], op=ADD)
 
-        def store_y(s):
+        def store_y(s, count=1):
             j = ORDER[s]
-            nc.sync.dma_start(out=out_0[P * j : P * (j + 1), :], in_=y[s][:])
+            nc.sync.dma_start(
+                out=out_0[P * j : P * (j + count), :].rearrange("(h p) u -> p h u", p=P),
+                in_=y_all[:, U * j : U * (j + count)].rearrange("p (h u) -> p h u", u=U),
+            )
 
         def by_pairs(ap):
             return ap.rearrange("p (q e b) -> p e q b", e=2, b=2)
 
         def round_y(s, eng_copy):
             y_bf[s] = keep.tile([P, U], BF16, name="ybf%d" % s)
-            eng_copy(out=y_bf[s][:].rearrange("p (e q b) -> p e q b", e=2, b=2), in_=by_pairs(y[s][:]))
+            eng_copy(out=y_bf[s][:].rearrange("p (e q b) -> p e q b", e=2, b=2), in_=by_pairs(y[s]))
 
         def round_from_psum(s):
             y_bf[s] = keep.tile([P, U], BF16, name="ybf%d" % s)
@@ -200,7 +214,8 @@ def tile_mimo_loaded_gram_k2_kernel(tc, h_words, h_scales, h_stack, load, col_sc
                     nc.tensor.transpose(turned[m][:, h, e, :], words[:, P * e : P * (e + 1)], ident[:])
 
         def pack(m, eng_copy):
-            dst = packed[:, 4 * P * m : 4 * P * (m + 1)].rearrange("p (h i e) -> p h i e", h=2, e=2)
+            j = ORDER[2 * m]
+            dst = packed[:, 2 * P * j : 2 * P * (j + 2)].rearrange("p (h i e) -> p h i e", h=2, e=2)
             eng_copy(out=dst, in_=turned[m][:].rearrange("p h e i -> p h i e"))
 
         def quantise_y(j0, j1):
@@ -210,20 +225,23 @@ def tile_mimo_loaded_gram_k2_kernel(tc, h_words, h_scales, h_stack, load, col_sc
                 scales=out_scales[:, cols],
                 in_=packed[:, 2 * P * j0 : 2 * P * j1].bitcast(BF16),
             )
+
+        def store_codes(j0, j1):
+            cols = slice(P * j0, P * j1)
             dst = out_1[0].rearrange("p n t -> p (n t)").bitcast(I32)
             nc.sync.dma_start(out=dst[:, cols], in_=out_codes[:, cols].bitcast(I32))
 
         finish(0)
         finish(1)
         scale(0)
+        store_y(0)
         finish(2)
         scale(1)
+        store_y(1)
         round_y(0, nc.scalar.copy)
-        store_y(0)
         finish(3)
         scale(2)
         round_y(1, nc.scalar.copy)
-        store_y(1)
         finish(4)
         scale(3)
         round_y(2, nc.scalar.copy)
@@ -240,9 +258,8 @@ def tile_mimo_loaded_gram_k2_kernel(tc, h_words, h_scales, h_stack, load, col_sc
         finish(7)
         scale(6)
         round_y(5, nc.scalar.copy)
-        store_y(6)
         scale(7)
-        store_y(7)
+        store_y(6, 2)
         round_y(6, nc.vector.tensor_copy)
         round_y(7, nc.vector.tensor_copy)
         turn(0)
@@ -253,9 +270,12 @@ def tile_mimo_loaded_gram_k2_kernel(tc, h_words, h_scales, h_stack, load, col_sc
         pack(1, nc.scalar.copy)
         pack(2, nc.vector.tensor_copy)
         pack(3, nc.scalar.copy)
-        quantise_y(0, 4)
-        quantise_y(4, 6)
+        quantise_y(2, 6)
+        store_codes(2, 6)
+        quantise_y(0, 2)
+        store_codes(0, 2)
         quantise_y(6, 8)
+        store_codes(6, 8)
         rows = out_2[0].rearrange("(q r) n -> r q n", r=4)
         for r in range(4):
             queue = nc.sync if r < 2 else nc.scalar

from contextlib import ExitStack

import concourse.mybir as mybir
from concourse.masks import make_identity

K, U, R = 4096, 512, 1024
FLOPS = 2 * K * U * R

F32 = mybir.dt.float32
BF16 = mybir.dt.bfloat16
I32 = mybir.dt.int32
U32 = mybir.dt.uint32
U8 = mybir.dt.uint8
E4M3X4 = mybir.dt.float8_e4m3fn_x4
E5M2X4 = mybir.dt.float8_e5m2_x4
MULT = mybir.AluOpType.mult
ADD = mybir.AluOpType.add

P = 128
PACK = 4
PASSES = K // (P * PACK)
TILES = R // P
WIDE = 6
SCALE_RUNS = ((0, 2), (2, 4), (4, 6), (6, 8))
VECTOR_COLS = 336
ORDER = (4, 5, 2, 3, 0, 1, 6, 7)


def tile_mimo_loaded_gram_k2_kernel(tc, h_words, h_scales, h_stack, load, col_scale, out_0, out_1, out_2):
    nc = tc.nc
    with ExitStack() as ctx:
        keep = ctx.enter_context(tc.tile_pool(name="keep", bufs=1))
        stage = ctx.enter_context(tc.tile_pool(name="stage", bufs=3))
        psum = ctx.enter_context(tc.psum_pool(name="psum", bufs=1))
        ctx.enter_context(tc.manual_schedule())

        cs_in = keep.tile([P, PACK], BF16, name="cs_in")
        load_in = keep.tile([P, PACK], BF16, name="load_in")
        nc.scalar.dma_start(out=cs_in[:], in_=col_scale.rearrange("(p c) -> p c", c=PACK))
        nc.scalar.dma_start(out=load_in[:], in_=load.rearrange("(p c) -> p c", c=PACK))

        ident_bf = keep.tile([P, P], BF16, name="ident_bf")
        ident = keep.tile([P, P], F32, name="ident")
        make_identity(nc, ident_bf[:])
        nc.scalar.copy(out=ident[:], in_=ident_bf[:])

        planes = {}
        for g0, g1 in SCALE_RUNS:
            planes[g0] = keep.tile([P, g1 - g0, R], U8, name="plane%d" % g0, align_bytes=64)
            nc.vector.memset(planes[g0][:].bitcast(I32), 0)

        raw = {}
        hw = {}
        hw_tail = {}

        def load_stack(g):
            raw[g] = keep.tile([P, PACK, U], BF16, name="raw%d" % g)
            nc.sync.dma_start(out=raw[g][:], in_=h_stack[512 * g : 512 * (g + 1), :].rearrange("(p t) u -> p t u", t=PACK))

        def load_words(g, lo=0, hi=R):
            if lo == 0:
                hw[g] = keep.tile([P, R], U32, name="hw%d" % g, align_bytes=64)
            src = h_words[g].rearrange("p n t -> p (n t)").bitcast(I32)
            nc.sync.dma_start(out=hw[g][:, lo:hi].bitcast(I32), in_=src[:, lo:hi])

        def load_tail(j0, j1):
            words = keep.tile([P, PASSES - WIDE, P * (j1 - j0)], U32, name="hwt%d" % j0, align_bytes=64)
            src = h_words[WIDE:PASSES, :, P * j0 : P * j1, :].rearrange("g p n t -> p g (n t)").bitcast(I32)
            nc.sync.dma_start(out=words[:].bitcast(I32), in_=src)
            for j in range(j0, j1):
                hw_tail[j] = words[:, :, P * (j - j0) : P * (j - j0 + 1)]

        def load_scales(plane, g0, g1):
            rows = h_scales[g0:g1].rearrange("g (q r) n -> r q g n", r=4)
            for r in range(4):
                nc.sync.dma_start(out=plane[r:P:32, :, :].bitcast(I32), in_=rows[r].bitcast(I32))

        load_stack(0)
        load_words(0)
        load_stack(1)
        for g0, g1 in SCALE_RUNS[:-1]:
            load_scales(planes[g0], g0, g1)
        load_words(1)
        for g in range(2, WIDE - 1):
            load_stack(g)
            load_words(g)
        load_stack(WIDE - 1)
        load_stack(WIDE)
        load_words(WIDE - 1)
        load_stack(WIDE + 1)
        load_scales(planes[WIDE], WIDE, PASSES)
        for s in range(0, TILES, 2):
            load_tail(ORDER[s], ORDER[s] + 2)

        cs32 = keep.tile([P, PACK], F32, name="cs32")
        lc32 = keep.tile([P, PACK], F32, name="lc32")
        nc.vector.tensor_copy(out=cs32[:], in_=cs_in[:])
        nc.vector.tensor_tensor(out=lc32[:], in0=cs_in[:], in1=load_in[:], op=MULT)
        cs_ps = psum.tile([P, PACK, P], F32, name="cs_ps", tag="bank6")
        lc_ps = psum.tile([P, PACK, P], F32, name="lc_ps", tag="bank7")
        for c in range(PACK):
            nc.tensor.transpose(cs_ps[:, c, :], cs32[:, c : c + 1].to_broadcast([P, P]), ident[:])
        for c in range(PACK):
            nc.tensor.transpose(lc_ps[:, c, :], lc32[:, c : c + 1].to_broadcast([P, P]), ident[:])
        cs_all = keep.tile([P, U], F32, name="cs_all")
        diag = keep.tile([P, PACK, P], F32, name="diag")

        codes = {}
        scales = {}

        def quantise_stack(g):
            grouped = stage.tile([P, U, PACK], BF16, name="grouped", align_bytes=64)
            shares = (
                (nc.vector.tensor_copy, 0, U // 2),
                (nc.vector.tensor_copy, U // 2, VECTOR_COLS),
                (nc.scalar.copy, VECTOR_COLS, U),
            )
            for eng_copy, lo, hi in shares:
                eng_copy(
                    out=grouped[:, lo:hi, :].rearrange("p (c i) t -> p c t i", i=4),
                    in_=raw[g][:, :, lo:hi].rearrange("p t (c i) -> p c t i", i=4),
                )
            codes[g] = keep.tile([P, U], U32, name="codes%d" % g, align_bytes=64)
            scales[g] = keep.tile([P, U], U8, name="scales%d" % g, align_bytes=64)
            for lo, hi in ((0, U // 2), (U // 2, U)):
                nc.vector.quantize_mx(
                    out=codes[g][:, lo:hi].bitcast(E4M3X4),
                    scales=scales[g][:, lo:hi],
                    in_=grouped[:, lo:hi, :].rearrange("p u t -> p (u t)"),
                )

        acc = {}

        def multiply(s, g):
            j = ORDER[s]
            if g == 0:
                acc[s] = psum.tile([P, U], F32, name="acc%d" % s, tag="bank%d" % s)
            if g < WIDE:
                words = hw[g][:, P * j : P * (j + 1)]
            else:
                words = hw_tail[j][:, g - WIDE, :]
            first = max(g0 for g0, g1 in SCALE_RUNS if g0 <= g)
            plane = planes[first][:, g - first, :]
            nc.tensor.matmul_mx(
                out=acc[s][:],
                lhsT=words.bitcast(E5M2X4),
                lhsT_scale=plane[:, P * j : P * (j + 1)],
                rhs=codes[g][:].bitcast(E4M3X4),
                rhs_scale=scales[g][:],
                start=(g == 0),
                stop=(g == PASSES - 1),
            )

        quantise_stack(0)
        nc.scalar.copy(out=cs_all[:].rearrange("p (q c) -> p q c", c=PACK), in_=cs_ps[:].rearrange("p c q -> p q c"))
        nc.vector.tensor_tensor(
            out=diag[:].rearrange("p j (q c) -> p j q c", c=PACK),
            in0=lc_ps[:].rearrange("p c (j q) -> p j q c", j=PACK),
            in1=ident[:].rearrange("p (q c) -> p q c", c=PACK).unsqueeze(1).to_broadcast([P, PACK, P // PACK, PACK]),
            op=MULT,
        )
        for g in range(WIDE):
            if g > 0:
                quantise_stack(g)
            for j in range(TILES):
                multiply(ORDER.index(j), g)
        for g in range(WIDE, PASSES):
            quantise_stack(g)

        y_all = keep.tile([P, R // P * U], F32, name="y_all")
        y = {s: y_all[:, U * ORDER[s] : U * (ORDER[s] + 1)] for s in range(TILES)}
        y_bf = {}
        out_codes = keep.tile([P, R], U32, name="out_codes", align_bytes=64)
        out_scales = keep.tile([P, R], U8, name="out_scales", align_bytes=64)
        turned = {}
        packed = keep.tile([P, 2 * R], F32, name="packed", align_bytes=64)

        def finish(s):
            for g in range(WIDE, PASSES):
                multiply(s, g)

        def scale(s):
            j = ORDER[s]
            nc.vector.tensor_tensor(out=y[s], in0=acc[s][:], in1=cs_all[:], op=MULT)
            if j < PACK:
                block = y[s][:, P * j : P * (j + 1)]
                nc.gpsimd.tensor_tensor(out=block, in0=block, in1=diag[:, j, :], op=ADD)

        def store_y(s, count=1):
            j = ORDER[s]
            nc.sync.dma_start(
                out=out_0[P * j : P * (j + count), :].rearrange("(h p) u -> p h u", p=P),
                in_=y_all[:, U * j : U * (j + count)].rearrange("p (h u) -> p h u", u=U),
            )

        def by_pairs(ap):
            return ap.rearrange("p (q e b) -> p e q b", e=2, b=2)

        def round_y(s, eng_copy):
            y_bf[s] = keep.tile([P, U], BF16, name="ybf%d" % s)
            eng_copy(out=y_bf[s][:].rearrange("p (e q b) -> p e q b", e=2, b=2), in_=by_pairs(y[s]))

        def round_from_psum(s):
            y_bf[s] = keep.tile([P, U], BF16, name="ybf%d" % s)
            nc.vector.tensor_tensor(
                out=y_bf[s][:].rearrange("p (e q b) -> p e q b", e=2, b=2), in0=by_pairs(acc[s][:]), in1=by_pairs(cs_all[:]), op=MULT
            )

        def turn(m):
            turned[m] = psum.tile([P, 2, 2, P], F32, name="turned%d" % m, tag="bank%d" % (2 * m))
            for h in range(2):
                words = y_bf[2 * m + h][:].bitcast(F32)
                for e in range(2):
                    nc.tensor.transpose(turned[m][:, h, e, :], words[:, P * e : P * (e + 1)], ident[:])

        def pack(m, eng_copy):
            j = ORDER[2 * m]
            dst = packed[:, 2 * P * j : 2 * P * (j + 2)].rearrange("p (h i e) -> p h i e", h=2, e=2)
            eng_copy(out=dst, in_=turned[m][:].rearrange("p h e i -> p h i e"))

        def quantise_y(j0, j1):
            cols = slice(P * j0, P * j1)
            nc.vector.quantize_mx(
                out=out_codes[:, cols].bitcast(E4M3X4),
                scales=out_scales[:, cols],
                in_=packed[:, 2 * P * j0 : 2 * P * j1].bitcast(BF16),
            )

        def store_codes(j0, j1):
            cols = slice(P * j0, P * j1)
            dst = out_1[0].rearrange("p n t -> p (n t)").bitcast(I32)
            nc.sync.dma_start(out=dst[:, cols], in_=out_codes[:, cols].bitcast(I32))

        finish(0)
        finish(1)
        scale(0)
        store_y(0)
        finish(2)
        scale(1)
        store_y(1)
        round_y(0, nc.scalar.copy)
        finish(3)
        scale(2)
        round_y(1, nc.scalar.copy)
        finish(4)
        scale(3)
        round_y(2, nc.scalar.copy)
        store_y(2)
        finish(5)
        scale(4)
        round_y(3, nc.scalar.copy)
        store_y(3)
        store_y(4)
        finish(6)
        scale(5)
        round_y(4, nc.scalar.copy)
        store_y(5)
        finish(7)
        scale(6)
        round_y(5, nc.scalar.copy)
        scale(7)
        store_y(6, 2)
        round_y(6, nc.vector.tensor_copy)
        round_y(7, nc.vector.tensor_copy)
        turn(0)
        turn(1)
        turn(2)
        turn(3)
        pack(0, nc.scalar.copy)
        pack(1, nc.scalar.copy)
        pack(2, nc.vector.tensor_copy)
        pack(3, nc.scalar.copy)
        quantise_y(2, 6)
        store_codes(2, 6)
        quantise_y(0, 2)
        store_codes(0, 2)
        quantise_y(6, 8)
        store_codes(6, 8)
        rows = out_2[0].rearrange("(q r) n -> r q n", r=4)
        for r in range(4):
            queue = nc.sync if r < 2 else nc.scalar
            queue.dma_start(out=rows[r].bitcast(I32), in_=out_scales[r:P:32, :].bitcast(I32))
